import numpy as np
CORES = [0,1,2,3,4,5,6,7]
N = 8
GROUPS = [[0,2,4,6],[1,3,5,7]]
def setup_inputs(rng):
    return {"x": rng.standard_normal((N, 128, 512), dtype=np.float32)}
def reference(x):
    y = np.empty((N, 128, 128), x.dtype)
    for g in GROUPS:
        s = x[g].sum(axis=0, dtype=np.float64).astype(x[g].dtype)
        n = len(g); b = x.shape[2] // n
        for i, r in enumerate(g):
            y[r] = s[:, i * b:(i + 1) * b]
    return {"y": y}

from concourse.bass import DstId, RemoteDMATransfer
from concourse.mybir import AluOpType

P = 128
W = 128
NB = 4

SCRATCH = {
    "xs": ("sbuf", [P, NB * W], "float32"),
    "land1": ("sbuf", [P, 2 * W], "float32"),
    "land2": ("sbuf", [P, W], "float32"),
}
SEMAPHORES = ["loaded", "seeded", "arr1", "arr2", "sent", "acc"]


def rank_program(g, core, T, topo):
    rank = T.rank_of(core)
    if rank is None:
        return
    group = [grp for grp in T.tables["GROUPS"] if rank in grp][0]
    members = [T.cores[r] for r in group]
    mine = [c for c in members if topo.die(c) == topo.die(core)]
    far = [c for c in members if topo.die(c) != topo.die(core)]
    k = mine.index(core)
    partner = mine[1 - k]
    ward, partner_ward = far[k], far[1 - k]

    def blk(c):
        b = members.index(c)
        return slice(b * W, (b + 1) * W)

    def dst(c):
        rid, pid, _se = topo.addr(c)
        return DstId(rid=rid, pnc=pid)

    s = T.sem
    g.sync.dma_start(T.xs[:], T.x[:]).then_inc(s.loaded, 16)
    g.scalar.dma_start(T.y[:], T.x[:, blk(core)]).then_inc(s.seeded, 16)

    g.wait_ge(s.loaded, 16)
    g.remote_dma_fused(
        [
            RemoteDMATransfer(dst_ids=[dst(partner)], dma_engine_mask=0x00FF, remote_sem=s.arr1,
                              src=T.xs[:, blk(partner)], dst=T.land1[:, 0:W]),
            RemoteDMATransfer(dst_ids=[dst(partner)], dma_engine_mask=0xFF00, remote_sem=s.arr1,
                              src=T.xs[:, blk(partner_ward)], dst=T.land1[:, W:2 * W]),
        ],
        local_sem=s.sent,
    )

    g.wait_ge(s.arr1, 16)
    g.remote_dma_fused(
        [
            RemoteDMATransfer(dst_ids=[dst(ward)], dma_engine_mask=0xFFFF, remote_sem=s.arr2,
                              srcs=[T.xs[:, blk(ward)], T.land1[:, W:2 * W]], dsts=[T.land2[:]], alu_op=1),
        ],
        local_sem=s.sent,
    )

    g.wait_ge(s.seeded, 16)
    g.dma_start(T.y[:], T.land1[:, 0:W], accum_op=AluOpType.add).then_inc(s.acc, 16)
    g.wait_ge(s.acc, 16)
    g.wait_ge(s.arr2, 16)
    g.dma_start(T.y[:], T.land2[:], accum_op=AluOpType.add).then_inc(s.acc, 16)
    g.wait_ge(s.acc, 32)
    g.wait_ge(s.sent, 32)
